import numpy as np
import ml_dtypes


def mxq(x, axis, fmt="e4m3"):
    dtype, down = {"e4m3": (ml_dtypes.float8_e4m3fn, 7), "e5m2": (ml_dtypes.float8_e5m2, 14)}[fmt]
    v = np.moveaxis(np.asarray(x, np.float32).astype(ml_dtypes.bfloat16).astype(np.float64), axis, -1)
    blocks = v.reshape(v.shape[:-1] + (-1, 32))
    amax = np.abs(blocks).max(-1, keepdims=True)
    byte = np.maximum(np.where(amax > 0, np.frexp(amax)[1] - 1 + 127, 0) - down, 1)
    scale = np.exp2(byte - 127.0)
    codes = (blocks / scale).astype(np.float32).astype(dtype).astype(np.float64)
    return np.moveaxis((codes * scale).reshape(v.shape), -1, axis)


WIDE = False


def mx_kscale(k):
    if not WIDE:
        return np.ones(k)
    levels = np.array([10, -10, 5, -5, 0])
    if k % 512:
        return np.exp2(np.random.permutation(np.resize(levels, k // 32))).repeat(32)
    a = np.empty((k // 512, 16))
    for p in range(k // 512):
        a[p, :8] = np.random.permutation(np.resize(levels, 8))
        for g in range(8):
            far = levels[np.abs(levels - a[p, g]) >= 10]
            a[p, g + 8] = far[np.random.randint(len(far))]
    return np.exp2(a.ravel()).repeat(32)


def f64(x):
    return np.asarray(x).astype(np.float64)


def striped(idx):
    return np.tile(idx.reshape(-1, 16).T, (8, 1)).astype(np.uint16)


def unstriped(offs):
    return offs[:16].T.reshape(-1).astype(np.int64)


def pack_weight(w):
    k, n = w.shape
    w = f64(np.asarray(w, np.float32).astype(ml_dtypes.bfloat16)).reshape(k // 32, 32, n)
    amax = np.abs(w).max(1)
    byte = np.clip(np.where(amax > 0, np.frexp(amax)[1] - 1 + 127 - 7, 1), 1, 254)
    scaled = (w * np.exp2(127.0 - byte)[:, None, :]).reshape(k, n).astype(np.float32)
    words = np.ascontiguousarray(scaled.reshape(k // 512, 128, 4, n).transpose(0, 1, 3, 2)).astype(ml_dtypes.float8_e4m3fn).view(np.uint8)
    return words, np.ascontiguousarray(byte.astype(np.uint8).reshape(k // 512, 16, n))


def unpack_weight(words, scales):
    g, p, n, _ = words.shape
    vals = np.ascontiguousarray(words).view(ml_dtypes.float8_e4m3fn).astype(np.float64) * np.repeat(np.exp2(scales.astype(np.float64) - 127.0), 8, axis=1)[..., None]
    return vals.transpose(0, 1, 3, 2).reshape(g * 512, n)


def gelu(v):
    return 0.5 * v * (1.0 + np.tanh(np.sqrt(2.0 / np.pi) * (v + 0.044715 * v**3)))


K, T, D, S, V, N = 1024, 2048, 8, 1280, 160, 128


def setup_inputs():
    n = np.random.standard_normal
    s = mx_kscale(K)[:, None]
    packed = pack_weight(n((K, T)) * s)
    return {
        "x_words": packed[0],
        "x_scales": packed[1],
        "w": (n((K, N)) / np.sqrt(K) / s).astype(np.float32),
        "b": (0.3 * n((N, 1))).astype(np.float32),
        "offs": striped(np.random.permutation(T)[:S]),
    }


def reference(x_words, x_scales, w, b, offs):
    idx = unstriped(offs)
    xq = unpack_weight(x_words, x_scales)[:, idx]
    y = mxq(f64(w), 0, "e4m3").T @ xq
    y = gelu(y + f64(b))
    return y.reshape(N, V, D).max(axis=2)

@@ -1,0 +1,115 @@
+from contextlib import ExitStack
+
+import concourse.mybir as mybir
+
+K, T, D, S, V, N = 1024, 2048, 8, 1280, 160, 128
+FLOPS = 2 * K * S * N
+
+F32 = mybir.dt.float32
+BF16 = mybir.dt.bfloat16
+I32 = mybir.dt.int32
+U32 = mybir.dt.uint32
+U16 = mybir.dt.uint16
+U8 = mybir.dt.uint8
+FP8X4 = mybir.dt.float8_e4m3fn_x4
+
+P = 128
+PACK = 4
+PASSES = K // (P * PACK)
+LIST_ROWS = 16
+CHUNKS = ((0, 512), (512, 1024), (1024, 1280))
+
+
+def tile_picked_pool_lin_gelu_sub_p_kernel(tc, x_words, x_scales, w, b, offs, out):
+    nc = tc.nc
+    with ExitStack() as ctx:
+        keep = ctx.enter_context(tc.tile_pool(name="keep", bufs=1))
+        psum = ctx.enter_context(tc.psum_pool(name="psum", bufs=1))
+
+        offsets = keep.tile([P, S // LIST_ROWS], U16, name="offsets")
+        nc.sync.dma_start(offsets[:], offs)
+
+        scale_table = keep.tile([P, T], U8, name="scale_table", align_bytes=64)
+        nc.sync.dma_start(
+            scale_table[0:32, :].bitcast(I32),
+            x_scales.rearrange("o q c -> q o c").bitcast(I32),
+        )
+        nc.vector.memset(scale_table[32:64, :].bitcast(I32), 0)
+        nc.vector.memset(scale_table[64:P, :].bitcast(I32), 0)
+
+        word_tables = [keep.tile([P, T], I32, name="word_table%d" % o, align_bytes=64) for o in range(PASSES)]
+        w_raw = keep.tile([P, PASSES, PACK, N], F32, name="w_raw")
+        bias = keep.tile([P, 1], F32, name="bias")
+
+        def load_words(o):
+            nc.sync.dma_start(word_tables[o][:], x_words[o].rearrange("p c r -> p (c r)").bitcast(I32))
+
+        nc.sync.dma_start(
+            w_raw[:].rearrange("p o t n -> p o (t n)"),
+            w.rearrange("(o p t) n -> p o (t n)", o=PASSES, t=PACK),
+        )
+        load_words(0)
+        load_words(1)
+        nc.sync.dma_start(bias[:], b)
+
+        x_planes = keep.tile([P, S], U8, name="x_planes", align_bytes=64)
+
+        picked_scales = keep.tile([P, S], U8, name="picked_scales", align_bytes=64)
+        nc.vector.tensor_copy(picked_scales[:], scale_table[:].indirect(offsets[:]))
+        for j in range(4):
+            nc.sync.dma_start(
+                x_planes[j:P:4, :].bitcast(I32),
+                picked_scales[2 * j : 2 * j + 32, :].bitcast(I32),
+            )
+
+        w_grouped = keep.tile([P, PASSES, N, PACK], BF16, name="w_grouped", align_bytes=64)
+        nc.scalar.copy(out=w_grouped[:], in_=w_raw[:].rearrange("p o t n -> p o n t"))
+
+        picked = [keep.tile([P, S], U32, name="picked0", align_bytes=64)]
+        nc.vector.tensor_copy(picked[0][:], word_tables[0][:].bitcast(U32).indirect(offsets[:]))
+
+        w_codes = keep.tile([P, PASSES * N], U32, name="w_codes", align_bytes=64)
+        w_planes = keep.tile([P, PASSES * N], U8, name="w_planes", align_bytes=64)
+        nc.vector.quantize_mx(
+            out=w_codes[:].bitcast(FP8X4),
+            scales=w_planes[:],
+            in_=w_grouped[:].rearrange("p o n t -> p (o n t)"),
+        )
+
+        banks = [psum.tile([P, hi - lo], F32, name="bank%d" % c) for c, (lo, hi) in enumerate(CHUNKS)]
+
+        def multiply(o, c, words):
+            lo, hi = CHUNKS[c]
+            nc.tensor.matmul_mx(
+                out=banks[c][:],
+                lhsT=w_codes[:, o * N : (o + 1) * N].bitcast(FP8X4),
+                lhsT_scale=w_planes[:, o * N : (o + 1) * N],
+                rhs=words.bitcast(FP8X4),
+                rhs_scale=x_planes[4 * o : P, lo:hi],
+                start=(o == 0),
+                stop=(o == PASSES - 1),
+            )
+
+        for c, (lo, hi) in enumerate(CHUNKS):
+            multiply(0, c, picked[0][:, lo:hi])
+
+        activated = []
+        for c, (lo, hi) in enumerate(CHUNKS):
+            last = keep.tile([P, hi - lo], U32, name="picked1_%d" % c, align_bytes=64)
+            nc.vector.tensor_copy(
+                last[:], word_tables[1][:].bitcast(U32).indirect(offsets[:, lo // LIST_ROWS : hi // LIST_ROWS])
+            )
+            multiply(1, c, last[:])
+            y = keep.tile([P, hi - lo], F32, name="y%d" % c)
+            nc.scalar.activation(y[:], banks[c][:], mybir.ActivationFunctionType.Gelu_apprx_tanh, bias=bias[:])
+            activated.append(y)
+
+        pooled = keep.tile([P, V], F32, name="pooled")
+        for c, (lo, hi) in enumerate(CHUNKS):
+            nc.vector.tensor_reduce(
+                pooled[:, lo // D : hi // D],
+                activated[c][:].rearrange("p (v d) -> p v d", d=D),
+                mybir.AxisListType.X,
+                mybir.AluOpType.max,
+            )
+        nc.sync.dma_start(out, pooled[:])

@@ -38,17 +38,17 @@ def tile_picked_pool_lin_gelu_sub_p_kernel(tc, x_words, x_scales, w, b, offs, ou
         nc.vector.memset(scale_table[64:P, :].bitcast(I32), 0)
 
         word_tables = [keep.tile([P, T], I32, name="word_table%d" % o, align_bytes=64) for o in range(PASSES)]
-        w_raw = keep.tile([P, PASSES, PACK, N], F32, name="w_raw")
+        w_raw = keep.tile([P, PASSES, PACK, N], F32, name="w_raw", tag="w_then_words", align_bytes=64)
         bias = keep.tile([P, 1], F32, name="bias")
 
         def load_words(o):
             nc.sync.dma_start(word_tables[o][:], x_words[o].rearrange("p c r -> p (c r)").bitcast(I32))
 
+        load_words(0)
         nc.sync.dma_start(
             w_raw[:].rearrange("p o t n -> p o (t n)"),
             w.rearrange("(o p t) n -> p o (t n)", o=PASSES, t=PACK),
         )
-        load_words(0)
         load_words(1)
         nc.sync.dma_start(bias[:], b)
 
@@ -94,12 +94,12 @@ def tile_picked_pool_lin_gelu_sub_p_kernel(tc, x_words, x_scales, w, b, offs, ou
             multiply(0, c, picked[0][:, lo:hi])
 
         activated = []
+        last = keep.tile([P, S], U32, name="picked1", tag="w_then_words", align_bytes=64)
         for c, (lo, hi) in enumerate(CHUNKS):
-            last = keep.tile([P, hi - lo], U32, name="picked1_%d" % c, align_bytes=64)
             nc.vector.tensor_copy(
-                last[:], word_tables[1][:].bitcast(U32).indirect(offsets[:, lo // LIST_ROWS : hi // LIST_ROWS])
+                last[:, lo:hi], word_tables[1][:].bitcast(U32).indirect(offsets[:, lo // LIST_ROWS : hi // LIST_ROWS])
             )
-            multiply(1, c, last[:])
+            multiply(1, c, last[:, lo:hi])
             y = keep.tile([P, hi - lo], F32, name="y%d" % c)
             nc.scalar.activation(y[:], banks[c][:], mybir.ActivationFunctionType.Gelu_apprx_tanh, bias=bias[:])
             activated.append(y)
@@ -112,4 +112,6 @@ def tile_picked_pool_lin_gelu_sub_p_kernel(tc, x_words, x_scales, w, b, offs, ou
                 mybir.AxisListType.X,
                 mybir.AluOpType.max,
             )
-        nc.sync.dma_start(out, pooled[:])
+        split = CHUNKS[-1][0] // D
+        nc.sync.dma_start(out[:, :split], pooled[:, :split])
+        nc.sync.dma_start(out[:, split:], pooled[:, split:])

@@ -17,7 +17,8 @@ P = 128
 PACK = 4
 PASSES = K // (P * PACK)
 LIST_ROWS = 16
-CHUNKS = ((0, 512), (512, 1024), (1024, 1280))
+CHUNKS = ((0, 256), (256, 768), (768, 1024), (1024, 1280))
+GATHERS = ((0, 768), (768, 1024), (1024, 1280))
 
 
 def tile_picked_pool_lin_gelu_sub_p_kernel(tc, x_words, x_scales, w, b, offs, out):
@@ -27,13 +28,13 @@ def tile_picked_pool_lin_gelu_sub_p_kernel(tc, x_words, x_scales, w, b, offs, ou
         psum = ctx.enter_context(tc.psum_pool(name="psum", bufs=1))
 
         offsets = keep.tile([P, S // LIST_ROWS], U16, name="offsets")
-        nc.sync.dma_start(offsets[:], offs)
 
         scale_table = keep.tile([P, T], U8, name="scale_table", align_bytes=64)
         nc.sync.dma_start(
             scale_table[0:32, :].bitcast(I32),
             x_scales.rearrange("o q c -> q o c").bitcast(I32),
         )
+        nc.sync.dma_start(offsets[:], offs)
         nc.vector.memset(scale_table[32:64, :].bitcast(I32), 0)
         nc.vector.memset(scale_table[64:P, :].bitcast(I32), 0)
 
@@ -95,10 +96,11 @@ def tile_picked_pool_lin_gelu_sub_p_kernel(tc, x_words, x_scales, w, b, offs, ou
 
         activated = []
         last = keep.tile([P, S], U32, name="picked1", tag="w_then_words", align_bytes=64)
-        for c, (lo, hi) in enumerate(CHUNKS):
+        for lo, hi in GATHERS:
             nc.vector.tensor_copy(
                 last[:, lo:hi], word_tables[1][:].bitcast(U32).indirect(offsets[:, lo // LIST_ROWS : hi // LIST_ROWS])
             )
+        for c, (lo, hi) in enumerate(CHUNKS):
             multiply(1, c, last[:, lo:hi])
             y = keep.tile([P, hi - lo], F32, name="y%d" % c)
             nc.scalar.activation(y[:], banks[c][:], mybir.ActivationFunctionType.Gelu_apprx_tanh, bias=bias[:])

from contextlib import ExitStack

import concourse.mybir as mybir

K, T, D, S, V, N = 1024, 2048, 8, 1280, 160, 128
FLOPS = 2 * K * S * N

F32 = mybir.dt.float32
BF16 = mybir.dt.bfloat16
I32 = mybir.dt.int32
U32 = mybir.dt.uint32
U16 = mybir.dt.uint16
U8 = mybir.dt.uint8
FP8X4 = mybir.dt.float8_e4m3fn_x4

P = 128
PACK = 4
PASSES = K // (P * PACK)
LIST_ROWS = 16
CHUNKS = ((0, 256), (256, 768), (768, 1024), (1024, 1280))
GATHERS = ((0, 768), (768, 1024), (1024, 1280))


def tile_picked_pool_lin_gelu_sub_p_kernel(tc, x_words, x_scales, w, b, offs, out):
    nc = tc.nc
    with ExitStack() as ctx:
        keep = ctx.enter_context(tc.tile_pool(name="keep", bufs=1))
        psum = ctx.enter_context(tc.psum_pool(name="psum", bufs=1))

        offsets = keep.tile([P, S // LIST_ROWS], U16, name="offsets")

        scale_table = keep.tile([P, T], U8, name="scale_table", align_bytes=64)
        nc.sync.dma_start(
            scale_table[0:32, :].bitcast(I32),
            x_scales.rearrange("o q c -> q o c").bitcast(I32),
        )
        nc.sync.dma_start(offsets[:], offs)
        nc.vector.memset(scale_table[32:64, :].bitcast(I32), 0)
        nc.vector.memset(scale_table[64:P, :].bitcast(I32), 0)

        word_tables = [keep.tile([P, T], I32, name="word_table%d" % o, align_bytes=64) for o in range(PASSES)]
        w_raw = keep.tile([P, PASSES, PACK, N], F32, name="w_raw", tag="w_then_words", align_bytes=64)
        bias = keep.tile([P, 1], F32, name="bias")

        def load_words(o):
            nc.sync.dma_start(word_tables[o][:], x_words[o].rearrange("p c r -> p (c r)").bitcast(I32))

        load_words(0)
        nc.sync.dma_start(
            w_raw[:].rearrange("p o t n -> p o (t n)"),
            w.rearrange("(o p t) n -> p o (t n)", o=PASSES, t=PACK),
        )
        load_words(1)
        nc.sync.dma_start(bias[:], b)

        x_planes = keep.tile([P, S], U8, name="x_planes", align_bytes=64)

        picked_scales = keep.tile([P, S], U8, name="picked_scales", align_bytes=64)
        nc.vector.tensor_copy(picked_scales[:], scale_table[:].indirect(offsets[:]))
        for j in range(4):
            nc.sync.dma_start(
                x_planes[j:P:4, :].bitcast(I32),
                picked_scales[2 * j : 2 * j + 32, :].bitcast(I32),
            )

        w_grouped = keep.tile([P, PASSES, N, PACK], BF16, name="w_grouped", align_bytes=64)
        nc.scalar.copy(out=w_grouped[:], in_=w_raw[:].rearrange("p o t n -> p o n t"))

        picked = [keep.tile([P, S], U32, name="picked0", align_bytes=64)]
        nc.vector.tensor_copy(picked[0][:], word_tables[0][:].bitcast(U32).indirect(offsets[:]))

        w_codes = keep.tile([P, PASSES * N], U32, name="w_codes", align_bytes=64)
        w_planes = keep.tile([P, PASSES * N], U8, name="w_planes", align_bytes=64)
        nc.vector.quantize_mx(
            out=w_codes[:].bitcast(FP8X4),
            scales=w_planes[:],
            in_=w_grouped[:].rearrange("p o n t -> p (o n t)"),
        )

        banks = [psum.tile([P, hi - lo], F32, name="bank%d" % c) for c, (lo, hi) in enumerate(CHUNKS)]

        def multiply(o, c, words):
            lo, hi = CHUNKS[c]
            nc.tensor.matmul_mx(
                out=banks[c][:],
                lhsT=w_codes[:, o * N : (o + 1) * N].bitcast(FP8X4),
                lhsT_scale=w_planes[:, o * N : (o + 1) * N],
                rhs=words.bitcast(FP8X4),
                rhs_scale=x_planes[4 * o : P, lo:hi],
                start=(o == 0),
                stop=(o == PASSES - 1),
            )

        for c, (lo, hi) in enumerate(CHUNKS):
            multiply(0, c, picked[0][:, lo:hi])

        activated = []
        last = keep.tile([P, S], U32, name="picked1", tag="w_then_words", align_bytes=64)
        for lo, hi in GATHERS:
            nc.vector.tensor_copy(
                last[:, lo:hi], word_tables[1][:].bitcast(U32).indirect(offsets[:, lo // LIST_ROWS : hi // LIST_ROWS])
            )
        for c, (lo, hi) in enumerate(CHUNKS):
            multiply(1, c, last[:, lo:hi])
            y = keep.tile([P, hi - lo], F32, name="y%d" % c)
            nc.scalar.activation(y[:], banks[c][:], mybir.ActivationFunctionType.Gelu_apprx_tanh, bias=bias[:])
            activated.append(y)

        pooled = keep.tile([P, V], F32, name="pooled")
        for c, (lo, hi) in enumerate(CHUNKS):
            nc.vector.tensor_reduce(
                pooled[:, lo // D : hi // D],
                activated[c][:].rearrange("p (v d) -> p v d", d=D),
                mybir.AxisListType.X,
                mybir.AluOpType.max,
            )
        split = CHUNKS[-1][0] // D
        nc.sync.dma_start(out[:, :split], pooled[:, :split])
        nc.sync.dma_start(out[:, split:], pooled[:, split:])
